import numpy as np
import ml_dtypes

BF16 = ml_dtypes.bfloat16


def bf(x):
    return np.asarray(x, np.float32).astype(BF16)


def f32(x):
    return np.asarray(x, np.float32)


def f64(x):
    return np.asarray(x).astype(np.float64)


def striped(idx):
    return np.concatenate([l.reshape(-1, 16).T for l in idx])


def rows(idx, k):
    return np.tile(np.repeat(idx, 16, axis=0), (k // (16 * 8), 1))


def look(tab, idx):
    return np.take_along_axis(f64(tab), rows(idx, len(tab)), axis=1)


K, S, V, N = 256, 2048, 2048, 2048


def silu(v):
    return v / (1.0 + np.exp(-v))


def setup_inputs():
    return {"tab": f32(np.random.standard_normal((2, K, S))), "y": f32(np.random.standard_normal((K, V))), "offs": striped(np.stack([np.random.permutation(S)[:N] for _ in range(8)]))}


def reference(tab, y, offs):
    idx = np.stack([g.T.reshape(-1) for g in np.split(offs, 8)])
    x = (np.maximum(look(tab[0], idx), f64(y))) * (silu(look(tab[1], idx)))
    return x

@@ -1,0 +1,52 @@
+import concourse.mybir as mybir
+
+P = 128
+ROWS = 256
+PLACES = 2048
+N = 2048
+PIECE = 512
+PER_COLUMN = 16
+
+F32 = mybir.dt.float32
+U16 = mybir.dt.uint16
+MAX = mybir.AluOpType.max
+MULT = mybir.AluOpType.mult
+SILU = mybir.ActivationFunctionType.Silu
+
+BYTES = 4 * (2 * ROWS * PLACES + 2 * ROWS * N) + 2 * P * (N // PER_COLUMN)
+
+
+def tile_lookup_vg_maxsilu_out_kernel(tc, tab, y, offs, out):
+    nc = tc.nc
+    blocks = range(ROWS // P)
+    with (
+        tc.tile_pool(name="held", bufs=1) as held,
+        tc.tile_pool(name="work", bufs=len(blocks) * (N // PIECE)) as work,
+    ):
+        offsets = held.tile([P, N // PER_COLUMN], U16, name="offsets")
+        nc.sync.dma_start(offsets[:], offs)
+
+        values, stream, gates = [], [], []
+        for b in blocks:
+            rows = slice(b * P, (b + 1) * P)
+            values.append(held.tile([P, PLACES], F32, name=f"values{b}"))
+            stream.append(held.tile([P, N], F32, name=f"stream{b}"))
+            gates.append(held.tile([P, PLACES], F32, name=f"gates{b}"))
+            nc.sync.dma_start(values[b][:], tab[0, rows, :])
+            nc.sync.dma_start(stream[b][:], y[rows, :])
+            nc.sync.dma_start(gates[b][:], tab[1, rows, :])
+
+        for b in blocks:
+            rows = slice(b * P, (b + 1) * P)
+            for start in range(0, N, PIECE):
+                cols = slice(start, start + PIECE)
+                lists = offsets[:, start // PER_COLUMN : (start + PIECE) // PER_COLUMN]
+
+                larger = work.tile([P, PIECE], F32, name="larger")
+                nc.vector.tensor_tensor(larger[:], values[b][:].indirect(lists), stream[b][:, cols], MAX)
+                gate = work.tile([P, PIECE], F32, name="gate")
+                nc.scalar.activation(gate[:], gates[b][:].indirect(lists), SILU)
+
+                product = work.tile([P, PIECE], F32, name="product")
+                nc.vector.tensor_tensor(product[:], larger[:], gate[:], MULT)
+                nc.sync.dma_start(out[rows, cols], product[:])

@@ -5,6 +5,7 @@ ROWS = 256
 PLACES = 2048
 N = 2048
 PIECE = 512
+BEHIND = 2
 PER_COLUMN = 16
 
 F32 = mybir.dt.float32
@@ -19,34 +20,57 @@ BYTES = 4 * (2 * ROWS * PLACES + 2 * ROWS * N) + 2 * P * (N // PER_COLUMN)
 def tile_lookup_vg_maxsilu_out_kernel(tc, tab, y, offs, out):
     nc = tc.nc
     blocks = range(ROWS // P)
+    pieces = [(b, start) for b in blocks for start in range(0, N, PIECE)]
+    per_block = N // PIECE
     with (
         tc.tile_pool(name="held", bufs=1) as held,
-        tc.tile_pool(name="work", bufs=len(blocks) * (N // PIECE)) as work,
+        tc.tile_pool(name="work", bufs=per_block) as work,
     ):
         offsets = held.tile([P, N // PER_COLUMN], U16, name="offsets")
         nc.sync.dma_start(offsets[:], offs)
 
-        values, stream, gates = [], [], []
+        early = held.tile([P, 1], F32, name="early")
+        nc.vector.memset(early[:], 0.0)
+        early_silu = held.tile([P, 1], F32, name="early_silu")
+        nc.scalar.activation(early_silu[:], early[:], SILU)
+
+        values = [held.tile([P, PLACES], F32, name=f"values{b}") for b in blocks]
+        gates = [held.tile([P, PLACES], F32, name=f"gates{b}") for b in blocks]
+        stream = [held.tile([P, PIECE], F32, name=f"stream{k}") for k in range(len(pieces))]
+
+        def piece_of(array, k):
+            b, start = pieces[k]
+            return array[b * P : (b + 1) * P, start : start + PIECE]
+
         for b in blocks:
             rows = slice(b * P, (b + 1) * P)
-            values.append(held.tile([P, PLACES], F32, name=f"values{b}"))
-            stream.append(held.tile([P, N], F32, name=f"stream{b}"))
-            gates.append(held.tile([P, PLACES], F32, name=f"gates{b}"))
             nc.sync.dma_start(values[b][:], tab[0, rows, :])
-            nc.sync.dma_start(stream[b][:], y[rows, :])
+            first = b * per_block
+            middle = first + per_block // 2
+            for k in range(first, middle):
+                nc.sync.dma_start(stream[k][:], piece_of(y, k))
             nc.sync.dma_start(gates[b][:], tab[1, rows, :])
+            for k in range(middle, first + per_block):
+                nc.sync.dma_start(stream[k][:], piece_of(y, k))
 
-        for b in blocks:
-            rows = slice(b * P, (b + 1) * P)
-            for start in range(0, N, PIECE):
-                cols = slice(start, start + PIECE)
-                lists = offsets[:, start // PER_COLUMN : (start + PIECE) // PER_COLUMN]
+        def look_up(k):
+            b, start = pieces[k]
+            lists = offsets[:, start // PER_COLUMN : (start + PIECE) // PER_COLUMN]
+            larger = work.tile([P, PIECE], F32, name="larger")
+            nc.vector.tensor_tensor(larger[:], values[b][:].indirect(lists), stream[k][:], MAX)
+            gate = work.tile([P, PIECE], F32, name="gate")
+            nc.scalar.activation(gate[:], gates[b][:].indirect(lists), SILU)
+            return larger, gate
 
-                larger = work.tile([P, PIECE], F32, name="larger")
-                nc.vector.tensor_tensor(larger[:], values[b][:].indirect(lists), stream[b][:, cols], MAX)
-                gate = work.tile([P, PIECE], F32, name="gate")
-                nc.scalar.activation(gate[:], gates[b][:].indirect(lists), SILU)
+        def join(k, larger, gate):
+            product = stream[(k + BEHIND) % len(pieces)]
+            nc.vector.tensor_tensor(product[:], larger[:], gate[:], MULT)
+            nc.sync.dma_start(piece_of(out, k), product[:])
 
-                product = work.tile([P, PIECE], F32, name="product")
-                nc.vector.tensor_tensor(product[:], larger[:], gate[:], MULT)
-                nc.sync.dma_start(out[rows, cols], product[:])
+        looked_up = []
+        for k in range(len(pieces)):
+            looked_up.append(look_up(k))
+            if k >= BEHIND:
+                join(k - BEHIND, *looked_up[k - BEHIND])
+        for k in range(len(pieces) - BEHIND, len(pieces)):
+            join(k, *looked_up[k])

import concourse.mybir as mybir

P = 128
ROWS = 256
PLACES = 2048
N = 2048
PIECE = 512
BEHIND = 2
PER_COLUMN = 16

F32 = mybir.dt.float32
U16 = mybir.dt.uint16
MAX = mybir.AluOpType.max
MULT = mybir.AluOpType.mult
SILU = mybir.ActivationFunctionType.Silu

BYTES = 4 * (2 * ROWS * PLACES + 2 * ROWS * N) + 2 * P * (N // PER_COLUMN)


def tile_lookup_vg_maxsilu_out_kernel(tc, tab, y, offs, out):
    nc = tc.nc
    blocks = range(ROWS // P)
    pieces = [(b, start) for b in blocks for start in range(0, N, PIECE)]
    per_block = N // PIECE
    with (
        tc.tile_pool(name="held", bufs=1) as held,
        tc.tile_pool(name="work", bufs=per_block) as work,
    ):
        offsets = held.tile([P, N // PER_COLUMN], U16, name="offsets")
        nc.sync.dma_start(offsets[:], offs)

        early = held.tile([P, 1], F32, name="early")
        nc.vector.memset(early[:], 0.0)
        early_silu = held.tile([P, 1], F32, name="early_silu")
        nc.scalar.activation(early_silu[:], early[:], SILU)

        values = [held.tile([P, PLACES], F32, name=f"values{b}") for b in blocks]
        gates = [held.tile([P, PLACES], F32, name=f"gates{b}") for b in blocks]
        stream = [held.tile([P, PIECE], F32, name=f"stream{k}") for k in range(len(pieces))]

        def piece_of(array, k):
            b, start = pieces[k]
            return array[b * P : (b + 1) * P, start : start + PIECE]

        for b in blocks:
            rows = slice(b * P, (b + 1) * P)
            nc.sync.dma_start(values[b][:], tab[0, rows, :])
            first = b * per_block
            middle = first + per_block // 2
            for k in range(first, middle):
                nc.sync.dma_start(stream[k][:], piece_of(y, k))
            nc.sync.dma_start(gates[b][:], tab[1, rows, :])
            for k in range(middle, first + per_block):
                nc.sync.dma_start(stream[k][:], piece_of(y, k))

        def look_up(k):
            b, start = pieces[k]
            lists = offsets[:, start // PER_COLUMN : (start + PIECE) // PER_COLUMN]
            larger = work.tile([P, PIECE], F32, name="larger")
            nc.vector.tensor_tensor(larger[:], values[b][:].indirect(lists), stream[k][:], MAX)
            gate = work.tile([P, PIECE], F32, name="gate")
            nc.scalar.activation(gate[:], gates[b][:].indirect(lists), SILU)
            return larger, gate

        def join(k, larger, gate):
            product = stream[(k + BEHIND) % len(pieces)]
            nc.vector.tensor_tensor(product[:], larger[:], gate[:], MULT)
            nc.sync.dma_start(piece_of(out, k), product[:])

        looked_up = []
        for k in range(len(pieces)):
            looked_up.append(look_up(k))
            if k >= BEHIND:
                join(k - BEHIND, *looked_up[k - BEHIND])
        for k in range(len(pieces) - BEHIND, len(pieces)):
            join(k, *looked_up[k])
